import numpy as np
import ml_dtypes


def mxq(x, axis, fmt="e4m3"):
    dtype, down = {"e4m3": (ml_dtypes.float8_e4m3fn, 7), "e5m2": (ml_dtypes.float8_e5m2, 14)}[fmt]
    v = np.moveaxis(np.asarray(x, np.float32).astype(ml_dtypes.bfloat16).astype(np.float64), axis, -1)
    blocks = v.reshape(v.shape[:-1] + (-1, 32))
    amax = np.abs(blocks).max(-1, keepdims=True)
    byte = np.maximum(np.where(amax > 0, np.frexp(amax)[1] - 1 + 127, 0) - down, 1)
    scale = np.exp2(byte - 127.0)
    codes = (blocks / scale).astype(np.float32).astype(dtype).astype(np.float64)
    return np.moveaxis((codes * scale).reshape(v.shape), -1, axis)


WIDE = False


def mx_kscale(k):
    if not WIDE:
        return np.ones(k)
    levels = np.array([10, -10, 5, -5, 0])
    if k % 512:
        return np.exp2(np.random.permutation(np.resize(levels, k // 32))).repeat(32)
    a = np.empty((k // 512, 16))
    for p in range(k // 512):
        a[p, :8] = np.random.permutation(np.resize(levels, 8))
        for g in range(8):
            far = levels[np.abs(levels - a[p, g]) >= 10]
            a[p, g + 8] = far[np.random.randint(len(far))]
    return np.exp2(a.ravel()).repeat(32)


def f64(x):
    return np.asarray(x).astype(np.float64)


def striped(idx):
    return np.tile(np.asarray(idx).reshape(-1, 16).T, (8, 1)).astype(np.uint16)


def unstriped(offs):
    return offs[:16].T.reshape(-1).astype(np.int64)


E2M1 = np.array([0.0, 0.5, 1.0, 1.5, 2.0, 3.0, 4.0, 6.0, -0.0, -0.5, -1.0, -1.5, -2.0, -3.0, -4.0, -6.0])


def pack_weight(w, fmt):
    k, n = w.shape
    w = f64(np.asarray(w, np.float32).astype(ml_dtypes.bfloat16)).reshape(k // 32, 32, n)
    amax = np.abs(w).max(1)
    if fmt == "e4m3":
        byte = np.frexp(amax)[1] - 1 + 127 - 7
    else:
        mant, ex = np.frexp(amax / 6.0)
        byte = np.where(mant > 0.5, ex, ex - 1) + 127
    byte = np.clip(np.where(amax > 0, byte, 1), 1, 254)
    scaled = (w * np.exp2(127.0 - byte)[:, None, :]).reshape(k, n).astype(np.float32)
    by_word = np.ascontiguousarray(scaled.reshape(k // 512, 128, 4, n).transpose(0, 1, 3, 2))
    if fmt == "e4m3":
        words = by_word.astype(ml_dtypes.float8_e4m3fn).view(np.uint8)
    else:
        c = by_word.astype(ml_dtypes.float4_e2m1fn).view(np.uint8) & 0xF
        words = (c[..., 0::2] | (c[..., 1::2] << 4)).reshape(k // 512, 128, 2 * n)
    return np.ascontiguousarray(words), np.ascontiguousarray(byte.astype(np.uint8).reshape(k // 512, 16, n))


def unpack_weight(words, scales, fmt):
    g, _, n = scales.shape
    words = np.ascontiguousarray(words).reshape(g, 128, n, -1)
    if fmt == "e4m3":
        vals = words.view(ml_dtypes.float8_e4m3fn).astype(np.float64)
    else:
        nib = np.empty((g, 128, n, 4), np.uint8)
        nib[..., 0::2] = words & 0xF
        nib[..., 1::2] = words >> 4
        vals = E2M1[nib]
    vals = vals * np.repeat(np.exp2(scales.astype(np.float64) - 127.0), 8, axis=1)[..., None]
    return vals.transpose(0, 1, 3, 2).reshape(g * 512, n)


def bf(x):
    return np.asarray(x, np.float32).astype(ml_dtypes.bfloat16)


def planes(Y):
    r, m = Y.shape
    b = f64(bf(Y)).reshape(r // 32, 32, m)
    amax = np.abs(b).max(1)
    byte = np.clip(np.where(amax > 0, np.frexp(amax)[1] - 1 + 127 - 7, 1), 1, 254)
    codes = (b * np.exp2(127.0 - byte)[:, None, :]).reshape(r, m).astype(np.float32).astype(ml_dtypes.float8_e4m3fn).view(np.uint8)
    words = codes.reshape(r // 512, 128, 4, m).transpose(0, 1, 3, 2)
    return np.ascontiguousarray(words), np.ascontiguousarray(byte.astype(np.uint8).reshape(r // 512, 16, m))


D, T, I, Q, E, V, G, H = 512, 2048, 512, 256, 512, 32, 64, 32


def setup_inputs():
    n = np.random.standard_normal
    idx = np.random.permutation(T)[:I]
    fd = mx_kscale(D)
    fi = mx_kscale(I)
    keysp = pack_weight(n((D, T)) / fd[:, None], "e2m1")
    return {
        "query": (n((D, Q)) * 1.0 / np.sqrt(D) * fd[:, None]).astype(np.float32),
        "keys_words": keysp[0],
        "keys_scales": keysp[1],
        "lam": (np.random.uniform(0.7, 1.5, (1, Q))).astype(np.float32),
        "os": (np.random.uniform(4.0, 16.0, (1, I)) * fi).astype(np.float32),
        "vals": (n((E, T))).astype(np.float32),
        "vsc": (np.random.uniform(0.5, 2.0, (1, I)) / fi).astype(np.float32),
        "offs": striped(idx),
    }


def reference(query, keys_words, keys_scales, lam, os, vals, vsc, offs):
    idx = unstriped(offs)
    keysu = unpack_weight(keys_words, keys_scales, "e2m1")
    keysidxg = keysu[:, idx]
    queryq = mxq(f64(query), 0, "e4m3")
    a0 = keysidxg.T @ queryq
    ag = a0.reshape(I, V, Q // V).mean(axis=2)
    ar = np.repeat(ag, Q // V, axis=1)
    s0 = a0 * f64(lam) - np.square(a0 - ar)
    s = s0.T
    bm = s.reshape(Q, G, I // G).max(axis=2)
    bmr = np.repeat(bm, I // G, axis=1)
    p = np.exp(s - bmr)
    pg = p.reshape(Q, G, I // G).sum(axis=2)
    eg = np.exp(bm - np.max(bm, axis=1, keepdims=True))
    k0 = eg / np.sum(eg, axis=1, keepdims=True) / pg
    kr = np.repeat(k0, I // G, axis=1)
    w = p * kr
    wo1 = w * f64(os)
    wt1 = wo1.T
    vg = f64(vals)[:, idx].reshape(E, H, I // H).mean(axis=2)
    vgr = np.repeat(vg, I // H, axis=1)
    vd = (f64(vals)[:, idx] - vgr) * f64(vsc)
    vt1 = vd.T
    vt1q = mxq(vt1, 0, "e4m3")
    wt1q = mxq(wt1, 0, "e4m3")
    o = vt1q.T @ wt1q
    words, scales = planes(o)
    return o, words, scales

@@ -1,0 +1,318 @@
+from contextlib import ExitStack
+
+import concourse.mybir as mybir
+from concourse.masks import make_identity
+
+D, T, I, Q, E = 512, 2048, 512, 256, 512
+FLOPS = 2 * D * I * Q + 2 * I * E * Q
+
+F32 = mybir.dt.float32
+BF16 = mybir.dt.bfloat16
+I32 = mybir.dt.int32
+U32 = mybir.dt.uint32
+U16 = mybir.dt.uint16
+U8 = mybir.dt.uint8
+FP8X4 = mybir.dt.float8_e4m3fn_x4
+FP4X4 = mybir.dt.float4_e2m1fn_x4
+ALU = mybir.AluOpType
+ACT = mybir.ActivationFunctionType
+AX = mybir.AxisListType
+
+P = 128
+TINY = 1e-30
+
+
+def tile_attend_rowtypical_bestofruns_centredvalues_pl_kernel(
+    tc, query, keys_words, keys_scales, lam, slot_os, vals, vsc, offs, out_0, out_1, out_2
+):
+    nc = tc.nc
+    with ExitStack() as ctx:
+        keep = ctx.enter_context(tc.tile_pool(name="keep", bufs=1))
+        psum = ctx.enter_context(tc.psum_pool(name="psum", bufs=1))
+
+        def sb(name, shape, dtype):
+            return keep.tile(shape, dtype, name=name, align_bytes=64)
+
+        def bank(name, tag):
+            return psum.tile([P, 512], F32, name=name, tag=tag)
+
+        offsets = keep.tile([P, I // 16], U16, name="offsets")
+        nc.sync.dma_start(offsets[:], offs)
+        staged_bytes = sb("staged_bytes", [P, T // 4], I32)
+        for quad in range(4):
+            nc.sync.dma_start(
+                staged_bytes[32 * quad : 32 * quad + 4, :],
+                keys_scales[0, 4 * quad : 4 * quad + 4, :].bitcast(I32),
+            )
+        q_raw = sb("q_raw", [P, 4, Q], F32)
+        nc.sync.dma_start(q_raw[:], query.rearrange("(p j) q -> p j q", j=4))
+        key_words = sb("key_words", [P, T], U16)
+        nc.sync.dma_start(key_words[:].bitcast(I32), keys_words[0].bitcast(I32))
+        val_rows = vals.rearrange("(p t) n -> t p n", t=4)
+        val_pool = [sb("val_pool%d" % t, [P, T], F32) for t in range(4)]
+        nc.sync.dma_start(val_pool[0][:], val_rows[0])
+        lam2 = sb("lam2", [P, 2], F32)
+        nc.sync.dma_start(lam2[:], lam.rearrange("o (p h) -> (o p) h", h=2))
+        vsc4 = sb("vsc4", [P, 4], F32)
+        nc.sync.dma_start(vsc4[:], vsc.rearrange("o (p t) -> (o p) t", t=4))
+        for t in range(1, 4):
+            nc.sync.dma_start(val_pool[t][:], val_rows[t])
+        os4 = sb("os4", [P, 4], F32)
+        nc.sync.dma_start(os4[:], slot_os.rearrange("o (p t) -> (o p) t", t=4))
+
+        ident = sb("ident", [P, P], F32)
+        make_identity(nc, ident[:])
+
+        key_bytes = sb("key_bytes", [P, T], U8)
+        nc.vector.memset(key_bytes[:].bitcast(I32), 0)
+        warm_in = sb("warm_in", [P, 1], F32)
+        warm_out = sb("warm_out", [P, 1], F32)
+        nc.vector.memset(warm_in[:], 0.0)
+        nc.scalar.activation(warm_out[:], warm_in[:], ACT.Exp)
+
+        def turn(out, in_, start=True, stop=True):
+            nc.tensor.matmul(out, lhsT=in_, rhs=ident[:], is_transpose=True, start=start, stop=stop)
+
+        def quantise(name, grouped, width):
+            codes = sb(name + "_codes", [P, width], U32)
+            scales = sb(name + "_scales", [P, width], U8)
+            nc.vector.quantize_mx(out=codes[:].bitcast(FP8X4), scales=scales[:], in_=grouped)
+            return codes, scales
+
+        for quad in range(4):
+            rows = slice(32 * quad, 32 * quad + 4)
+            nc.vector.tensor_copy(key_bytes[rows, :].bitcast(I32), staged_bytes[rows, :])
+        kb_g = sb("kb_g", [P, I], U8)
+        nc.vector.tensor_copy(kb_g[:], key_bytes[:].indirect(offsets[:]))
+        kw_g = sb("kw_g", [P, I], U16)
+        nc.vector.tensor_copy(kw_g[:], key_words[:].indirect(offsets[:]))
+
+        q_bf = sb("q_bf", [P, Q, 4], BF16)
+        nc.scalar.copy(
+            q_bf[:].rearrange("p (c i) t -> p c t i", i=4),
+            q_raw[:].rearrange("p t (c i) -> p c t i", i=4),
+        )
+        q_codes, q_scales = quantise("q", q_bf[:].rearrange("p q t -> p (q t)"), Q)
+
+        a0_sb, neg_mean = [], []
+        for b in range(2):
+            a0 = bank("a0_%d" % b, "x%d" % b)
+            for k in range(2):
+                cols = slice(P * (2 * b + k), P * (2 * b + k + 1))
+                nc.tensor.matmul_mx(
+                    out=a0[:, Q * k : Q * (k + 1)],
+                    lhsT=kw_g[:, cols].bitcast(FP4X4),
+                    lhsT_scale=kb_g[:, cols],
+                    rhs=q_codes[:].bitcast(FP8X4),
+                    rhs_scale=q_scales[:],
+                    start=True,
+                    stop=True,
+                )
+            group_sum = sb("group_sum%d" % b, [P, 64], F32)
+            dealt = sb("a0_sb%d" % b, [P, 2, 2, P], F32)
+            if b == 1:
+                nc.scalar.copy(dealt[:], a0[:].rearrange("p (k m h) -> p k h m", k=2, h=2))
+            nc.vector.tensor_reduce(group_sum[:], a0[:].rearrange("p (v j) -> p v j", j=8), AX.X, ALU.add)
+            if b == 0:
+                first_bank, first_dealt = a0, dealt
+            else:
+                nc.scalar.copy(first_dealt[:], first_bank[:].rearrange("p (k m h) -> p k h m", k=2, h=2))
+            a0_sb.append(dealt)
+            neg_mean.append(group_sum)
+        for b in range(2):
+            spread = sb("neg_mean%d" % b, [P, 2 * P], F32)
+            nc.scalar.activation(
+                spread[:].rearrange("p (v j) -> p v j", j=4),
+                neg_mean[b][:].unsqueeze(2).to_broadcast([P, 64, 4]),
+                ACT.Copy,
+                scale=-0.125,
+            )
+            neg_mean[b] = spread
+
+        picked, neg_vmean, v_mx = {}, {}, {}
+
+        def gather_values(t):
+            picked[t] = sb("picked%d" % t, [P, I], F32)
+            nc.vector.tensor_copy(picked[t][:], val_pool[t][:].indirect(offsets[:]))
+
+        def mean_values(t):
+            stretch_sum = sb("stretch_sum%d" % t, [P, 32], F32)
+            nc.vector.tensor_reduce(stretch_sum[:], picked[t][:].rearrange("p (s j) -> p s j", j=16), AX.X, ALU.add)
+            neg_vmean[t] = sb("neg_vmean%d" % t, [P, P], F32)
+            nc.scalar.activation(
+                neg_vmean[t][:].rearrange("p (s j) -> p s j", j=4),
+                stretch_sum[:].unsqueeze(2).to_broadcast([P, 32, 4]),
+                ACT.Copy,
+                scale=-0.0625,
+            )
+
+        v_bf = {}
+
+        def centre_values(t, on_vector):
+            centred = bank("centred%d" % t, "v%d" % (t % 2))
+            for r in range(4):
+                turn(centred[:, P * r : P * (r + 1)], picked[t][:, r:I:4], start=(r == 0), stop=False)
+            for r in range(4):
+                turn(centred[:, P * r : P * (r + 1)], neg_vmean[t][:], start=False, stop=(r == 3))
+            v_bf[t] = sb("v_bf%d" % t, [P, P, 4], BF16)
+            if on_vector:
+                nc.vector.tensor_tensor(
+                    v_bf[t][:],
+                    centred[:].rearrange("p (r e) -> p e r", r=4),
+                    vsc4[:].unsqueeze(1).to_broadcast([P, P, 4]),
+                    ALU.mult,
+                )
+            else:
+                for r in range(4):
+                    nc.scalar.activation(
+                        v_bf[t][:, :, r], centred[:, P * r : P * (r + 1)], ACT.Copy, scale=vsc4[:, r : r + 1]
+                    )
+
+        def quantise_values(t):
+            v_mx[t] = quantise("v%d" % t, v_bf[t][:].rearrange("p e r -> p (e r)"), P)
+
+        den = sb("den", [P, 2, 64], F32)
+        run_top = sb("run_top", [P, 2, 64], F32)
+        plain, square, expd, row_sum, e_turned = {}, {}, {}, {}, {}
+
+        def turn_scores(h):
+            plain[h] = bank("plain%d" % h, "a%d" % h)
+            diff = bank("diff%d" % h, "d%d" % h)
+            for k in range(4):
+                turn(diff[:, P * k : P * (k + 1)], a0_sb[k // 2][:, k % 2, h, :], start=(k == 0), stop=False)
+            for k in range(4):
+                turn(
+                    diff[:, P * k : P * (k + 1)],
+                    neg_mean[k // 2][:, P * (k % 2) : P * (k % 2 + 1)],
+                    start=False,
+                    stop=(k == 3),
+                )
+            for k in range(4):
+                turn(plain[h][:, P * k : P * (k + 1)], a0_sb[k // 2][:, k % 2, h, :])
+            square[h] = sb("square%d" % h, [P, I], F32)
+            nc.scalar.activation(square[h][:], diff[:], ACT.Square)
+
+        def exp_scores(h):
+            score = sb("score%d" % h, [P, I], F32)
+            nc.vector.scalar_tensor_tensor(
+                score[:], plain[h][:], lam2[:, h : h + 1], square[h][:], ALU.mult, ALU.subtract
+            )
+            run_max = sb("run_max%d" % h, [P, 64], F32)
+            nc.vector.tensor_reduce(run_max[:], score[:].rearrange("p (g j) -> p g j", j=8), AX.X, ALU.max)
+            neg_max = sb("neg_max%d" % h, [P, 1], F32)
+            nc.vector.tensor_reduce(neg_max[:], run_max[:], AX.X, ALU.max, negate=True)
+            expd[h] = sb("expd%d" % h, [P, 4, P], F32)
+            nc.scalar.activation(
+                expd[h][:].rearrange("q r p -> q p r"),
+                score[:].rearrange("q (p r) -> q p r", r=4),
+                ACT.Exp,
+                bias=neg_max[:],
+            )
+            row_sum[h] = sb("row_sum%d" % h, [P, 1], F32)
+            nc.scalar.activation(run_top[:, h, :], run_max[:], ACT.Exp, bias=neg_max[:], accum_out=row_sum[h][:])
+
+        def sum_runs(h):
+            run_sum = sb("run_sum%d" % h, [P, 64], F32)
+            nc.vector.tensor_reduce(run_sum[:], expd[h][:].rearrange("q r (g c) -> q g r c", c=2), AX.XY, ALU.add)
+            nc.vector.tensor_scalar(den[:, h, :], run_sum[:], row_sum[h][:], TINY, ALU.mult, ALU.max)
+            e_turned[h] = bank("e_turned%d" % h, "d%d" % h)
+            for r in range(4):
+                turn(e_turned[h][:, P * r : P * (r + 1)], expd[h][:, r, :])
+
+        factor = sb("factor", [P, 4, Q], F32)
+
+        def run_shares():
+            inv = sb("inv", [P, P], F32)
+            nc.vector.reciprocal(inv[:], den[:].rearrange("q h g -> q (h g)"))
+            share = sb("share", [P, 2 * P], F32)
+            nc.vector.tensor_tensor(
+                share[:].rearrange("q (n c) -> q n c", c=2),
+                run_top[:].rearrange("q h g -> q (h g)").unsqueeze(2).to_broadcast([P, P, 2]),
+                inv[:].unsqueeze(2).to_broadcast([P, P, 2]),
+                ALU.mult,
+            )
+            share_t = bank("share_t", "a0")
+            for h in range(2):
+                turn(share_t[:, P * h : P * (h + 1)], share[:, P * h : P * (h + 1)])
+            for r in range(4):
+                nc.scalar.activation(factor[:, r, :], share_t[:, 0:Q], ACT.Copy, scale=os4[:, r : r + 1])
+
+        w_mx = {}
+
+        def weights(half):
+            w_bf = sb("w_bf%d" % half, [P, 2, 64, 4], BF16)
+            for h in range(2):
+                c0 = 64 * half
+                nc.vector.tensor_tensor(
+                    w_bf[:, h, :, :],
+                    e_turned[h][:].rearrange("p (r m) -> p m r", r=4)[:, c0 : c0 + 64, :],
+                    factor[:].rearrange("p r n -> p n r")[:, P * h + c0 : P * h + c0 + 64, :],
+                    ALU.mult,
+                )
+            return w_bf
+
+        turn_scores(0)
+        turn_scores(1)
+        gather_values(0)
+        mean_values(0)
+        gather_values(1)
+        exp_scores(0)
+        exp_scores(1)
+        centre_values(0, False)
+        mean_values(1)
+        sum_runs(0)
+        gather_values(2)
+        sum_runs(1)
+        centre_values(1, False)
+        run_shares()
+        mean_values(2)
+        gather_values(3)
+        mean_values(3)
+        centre_values(2, False)
+        w_bf = [weights(half) for half in range(2)]
+        for half in range(2):
+            w_mx[half] = quantise("w%d" % half, w_bf[half][:].rearrange("p h m r -> p (h m r)"), P)
+        for t in range(3):
+            quantise_values(t)
+        centre_values(3, True)
+        quantise_values(3)
+
+        o_codes = sb("o_codes", [P, Q], I32)
+        o_scales = sb("o_scales", [P, Q], U8)
+        out_rows = out_0.rearrange("(p t) q -> p t q", t=4)
+        for half in range(2):
+            acc = bank("acc%d" % half, "x%d" % half)
+            for t in range(4):
+                nc.tensor.matmul_mx(
+                    out=acc[:, P * t : P * (t + 1)],
+                    lhsT=v_mx[t][0][:].bitcast(FP8X4),
+                    lhsT_scale=v_mx[t][1][:],
+                    rhs=w_mx[half][0][:].bitcast(FP8X4),
+                    rhs_scale=w_mx[half][1][:],
+                    start=True,
+                    stop=True,
+                )
+            o_sb = sb("o_sb%d" % half, [P, 4, P], F32)
+            nc.scalar.copy(
+                o_sb[:].rearrange("p t (m h) -> p t m h", h=2),
+                acc[:].rearrange("p (t h m) -> p t m h", t=4, h=2),
+            )
+            cols = slice(P * half, P * (half + 1))
+            nc.sync.dma_start(out_rows[:, :, cols], o_sb[:])
+            o_bf = sb("o_bf%d" % half, [P, P, 4], BF16)
+            nc.vector.tensor_copy(
+                o_bf[:].rearrange("p (c i) t -> p c t i", i=4),
+                o_sb[:].rearrange("p t (c i) -> p c t i", i=4),
+            )
+            nc.vector.quantize_mx(
+                out=o_codes[:, cols].bitcast(FP8X4),
+                scales=o_scales[:, cols],
+                in_=o_bf[:].rearrange("p q t -> p (q t)"),
+            )
+        nc.sync.dma_start(out_1[0].rearrange("p c r -> p (c r)").bitcast(I32), o_codes[:])
+        for quad in range(4):
+            queue = nc.scalar if quad % 2 else nc.sync
+            queue.dma_start(
+                out_2[0, 4 * quad : 4 * quad + 4, :].bitcast(I32),
+                o_scales[32 * quad : 32 * quad + 4, :].bitcast(I32),
+            )

@@ -19,7 +19,8 @@ ACT = mybir.ActivationFunctionType
 AX = mybir.AxisListType
 
 P = 128
-TINY = 1e-30
+HUGE = 1e30
+POOL_TILES = ()
 
 
 def tile_attend_rowtypical_bestofruns_centredvalues_pl_kernel(
@@ -30,8 +31,8 @@ def tile_attend_rowtypical_bestofruns_centredvalues_pl_kernel(
         keep = ctx.enter_context(tc.tile_pool(name="keep", bufs=1))
         psum = ctx.enter_context(tc.psum_pool(name="psum", bufs=1))
 
-        def sb(name, shape, dtype):
-            return keep.tile(shape, dtype, name=name, align_bytes=64)
+        def sb(name, shape, dtype, after=None):
+            return keep.tile(shape, dtype, name=name, tag=after or name, align_bytes=64)
 
         def bank(name, tag):
             return psum.tile([P, 512], F32, name=name, tag=tag)
@@ -52,7 +53,8 @@ def tile_attend_rowtypical_bestofruns_centredvalues_pl_kernel(
         val_pool = [sb("val_pool%d" % t, [P, T], F32) for t in range(4)]
         nc.sync.dma_start(val_pool[0][:], val_rows[0])
         lam2 = sb("lam2", [P, 2], F32)
-        nc.sync.dma_start(lam2[:], lam.rearrange("o (p h) -> (o p) h", h=2))
+        with nc.allow_non_contiguous_dma(reason="one factor for each query row"):
+            nc.sync.dma_start(lam2[:], lam.rearrange("o (h p) -> (o p) h", h=2))
         vsc4 = sb("vsc4", [P, 4], F32)
         nc.sync.dma_start(vsc4[:], vsc.rearrange("o (p t) -> (o p) t", t=4))
         for t in range(1, 4):
@@ -73,8 +75,8 @@ def tile_attend_rowtypical_bestofruns_centredvalues_pl_kernel(
         def turn(out, in_, start=True, stop=True):
             nc.tensor.matmul(out, lhsT=in_, rhs=ident[:], is_transpose=True, start=start, stop=stop)
 
-        def quantise(name, grouped, width):
-            codes = sb(name + "_codes", [P, width], U32)
+        def quantise(name, grouped, width, after=None):
+            codes = sb(name + "_codes", [P, width], U32, after)
             scales = sb(name + "_scales", [P, width], U8)
             nc.vector.quantize_mx(out=codes[:].bitcast(FP8X4), scales=scales[:], in_=grouped)
             return codes, scales
@@ -84,8 +86,8 @@ def tile_attend_rowtypical_bestofruns_centredvalues_pl_kernel(
             nc.vector.tensor_copy(key_bytes[rows, :].bitcast(I32), staged_bytes[rows, :])
         kb_g = sb("kb_g", [P, I], U8)
         nc.vector.tensor_copy(kb_g[:], key_bytes[:].indirect(offsets[:]))
-        kw_g = sb("kw_g", [P, I], U16)
-        nc.vector.tensor_copy(kw_g[:], key_words[:].indirect(offsets[:]))
+        kw_g = [sb("kw_g0", [P, I // 2], U16)]
+        nc.vector.tensor_copy(kw_g[0][:], key_words[:].indirect(offsets[:, 0:16]))
 
         q_bf = sb("q_bf", [P, Q, 4], BF16)
         nc.scalar.copy(
@@ -93,51 +95,69 @@ def tile_attend_rowtypical_bestofruns_centredvalues_pl_kernel(
             q_raw[:].rearrange("p t (c i) -> p c t i", i=4),
         )
         q_codes, q_scales = quantise("q", q_bf[:].rearrange("p q t -> p (q t)"), Q)
+        kw_g.append(sb("kw_g1", [P, I // 2], U16, "q_bf"))
+        nc.vector.tensor_copy(kw_g[1][:], key_words[:].indirect(offsets[:, 16:32]))
 
-        a0_sb, neg_mean = [], []
-        for b in range(2):
-            a0 = bank("a0_%d" % b, "x%d" % b)
-            for k in range(2):
-                cols = slice(P * (2 * b + k), P * (2 * b + k + 1))
+        a0_banks, a0_sb, neg_mean, plain = {}, {}, {}, {}
+        for h in range(2):
+            a0_banks[h] = bank("a0_%d" % h, "x%d" % h)
+            for k in range(4):
                 nc.tensor.matmul_mx(
-                    out=a0[:, Q * k : Q * (k + 1)],
-                    lhsT=kw_g[:, cols].bitcast(FP4X4),
-                    lhsT_scale=kb_g[:, cols],
-                    rhs=q_codes[:].bitcast(FP8X4),
-                    rhs_scale=q_scales[:],
+                    out=a0_banks[h][:, P * k : P * (k + 1)],
+                    lhsT=kw_g[k // 2][:, P * (k % 2) : P * (k % 2 + 1)].bitcast(FP4X4),
+                    lhsT_scale=kb_g[:, P * k : P * (k + 1)],
+                    rhs=q_codes[:, P * h : P * (h + 1)].bitcast(FP8X4),
+                    rhs_scale=q_scales[:, P * h : P * (h + 1)],
                     start=True,
                     stop=True,
                 )
-            group_sum = sb("group_sum%d" % b, [P, 64], F32)
-            dealt = sb("a0_sb%d" % b, [P, 2, 2, P], F32)
-            if b == 1:
-                nc.scalar.copy(dealt[:], a0[:].rearrange("p (k m h) -> p k h m", k=2, h=2))
-            nc.vector.tensor_reduce(group_sum[:], a0[:].rearrange("p (v j) -> p v j", j=8), AX.X, ALU.add)
-            if b == 0:
-                first_bank, first_dealt = a0, dealt
-            else:
-                nc.scalar.copy(first_dealt[:], first_bank[:].rearrange("p (k m h) -> p k h m", k=2, h=2))
-            a0_sb.append(dealt)
-            neg_mean.append(group_sum)
+        plain[0] = bank("plain0", "a0")
         for b in range(2):
-            spread = sb("neg_mean%d" % b, [P, 2 * P], F32)
+            nc.tensor.matmul_mx(
+                out=plain[0][:, Q * b : Q * (b + 1)],
+                lhsT=q_codes[:, 0:P].bitcast(FP8X4),
+                lhsT_scale=q_scales[:, 0:P],
+                rhs=kw_g[b][:].bitcast(FP4X4),
+                rhs_scale=kb_g[:, Q * b : Q * (b + 1)],
+                start=True,
+                stop=True,
+            )
+
+        def copy_products(h):
+            a0_sb[h] = sb("a0_sb%d" % h, [P, I], F32)
+            nc.scalar.copy(a0_sb[h][:], a0_banks[h][:])
+
+        def group_means(h):
+            group_sum = sb("group_sum%d" % h, [P, 64], F32)
+            nc.vector.tensor_reduce(group_sum[:], a0_banks[h][:].rearrange("p (v j) -> p v j", j=8), AX.X, ALU.add)
+            neg_mean[h] = sb("neg_mean%d" % h, [P, I], F32)
             nc.scalar.activation(
-                spread[:].rearrange("p (v j) -> p v j", j=4),
-                neg_mean[b][:].unsqueeze(2).to_broadcast([P, 64, 4]),
+                neg_mean[h][:].rearrange("p (v j) -> p v j", j=8),
+                group_sum[:].unsqueeze(2).to_broadcast([P, 64, 8]),
                 ACT.Copy,
                 scale=-0.125,
             )
-            neg_mean[b] = spread
 
-        picked, neg_vmean, v_mx = {}, {}, {}
+        picked, neg_vmean, v_mx, v_bf = {}, {}, {}, {}
 
-        def gather_values(t):
-            picked[t] = sb("picked%d" % t, [P, I], F32)
+        def gather_values(t, after):
+            picked[t] = sb("picked%d" % t, [P, I], F32, after)
             nc.vector.tensor_copy(picked[t][:], val_pool[t][:].indirect(offsets[:]))
 
-        def mean_values(t):
-            stretch_sum = sb("stretch_sum%d" % t, [P, 32], F32)
-            nc.vector.tensor_reduce(stretch_sum[:], picked[t][:].rearrange("p (s j) -> p s j", j=16), AX.X, ALU.add)
+        def mean_values(t, after=None):
+            stretch_sum = sb("stretch_sum%d" % t, [P, 32], F32, after)
+            if t in POOL_TILES:
+                part = picked[t]
+                for width in (8, 4, 2, 1):
+                    halves = part[:].rearrange("p (s u j) -> p s u j", u=2, j=width)
+                    part = stretch_sum if width == 1 else sb("part%d_%d" % (t, width), [P, 32 * width], F32)
+                    nc.gpsimd.tensor_tensor(
+                        part[:].rearrange("p (s j) -> p s j", j=width), halves[:, :, 0, :], halves[:, :, 1, :], ALU.add
+                    )
+            else:
+                nc.vector.tensor_reduce(
+                    stretch_sum[:], picked[t][:].rearrange("p (s j) -> p s j", j=16), AX.X, ALU.add
+                )
             neg_vmean[t] = sb("neg_vmean%d" % t, [P, P], F32)
             nc.scalar.activation(
                 neg_vmean[t][:].rearrange("p (s j) -> p s j", j=4),
@@ -146,18 +166,16 @@ def tile_attend_rowtypical_bestofruns_centredvalues_pl_kernel(
                 scale=-0.0625,
             )
 
-        v_bf = {}
-
-        def centre_values(t, on_vector):
-            centred = bank("centred%d" % t, "v%d" % (t % 2))
+        def centre_values(t, tag, after, on_vector):
+            centred = bank("centred%d" % t, tag)
             for r in range(4):
                 turn(centred[:, P * r : P * (r + 1)], picked[t][:, r:I:4], start=(r == 0), stop=False)
             for r in range(4):
                 turn(centred[:, P * r : P * (r + 1)], neg_vmean[t][:], start=False, stop=(r == 3))
-            v_bf[t] = sb("v_bf%d" % t, [P, P, 4], BF16)
+            v_bf[t] = sb("v_bf%d" % t, [P, P, 4], BF16, after)[:]
             if on_vector:
                 nc.vector.tensor_tensor(
-                    v_bf[t][:],
+                    v_bf[t],
                     centred[:].rearrange("p (r e) -> p e r", r=4),
                     vsc4[:].unsqueeze(1).to_broadcast([P, P, 4]),
                     ALU.mult,
@@ -168,138 +186,176 @@ def tile_attend_rowtypical_bestofruns_centredvalues_pl_kernel(
                         v_bf[t][:, :, r], centred[:, P * r : P * (r + 1)], ACT.Copy, scale=vsc4[:, r : r + 1]
                     )
 
-        def quantise_values(t):
-            v_mx[t] = quantise("v%d" % t, v_bf[t][:].rearrange("p e r -> p (e r)"), P)
+        def quantise_values(t, after=None):
+            codes, scales = quantise("v%d" % t, v_bf[t].rearrange("p e r -> p (e r)"), P, after)
+            v_mx[t] = (codes[:], scales[:])
 
-        den = sb("den", [P, 2, 64], F32)
-        run_top = sb("run_top", [P, 2, 64], F32)
-        plain, square, expd, row_sum, e_turned = {}, {}, {}, {}, {}
+        square, score, run_max, neg_max, expd, run_top, e_turned, inv, share = {}, {}, {}, {}, {}, {}, {}, {}, {}
+        row_sum = sb("row_sum", [P, 2], F32)
 
-        def turn_scores(h):
-            plain[h] = bank("plain%d" % h, "a%d" % h)
+        def turn_differences(h):
             diff = bank("diff%d" % h, "d%d" % h)
             for k in range(4):
-                turn(diff[:, P * k : P * (k + 1)], a0_sb[k // 2][:, k % 2, h, :], start=(k == 0), stop=False)
+                turn(diff[:, P * k : P * (k + 1)], a0_sb[h][:, P * k : P * (k + 1)], start=(k == 0), stop=False)
             for k in range(4):
-                turn(
-                    diff[:, P * k : P * (k + 1)],
-                    neg_mean[k // 2][:, P * (k % 2) : P * (k % 2 + 1)],
-                    start=False,
-                    stop=(k == 3),
-                )
-            for k in range(4):
-                turn(plain[h][:, P * k : P * (k + 1)], a0_sb[k // 2][:, k % 2, h, :])
+                turn(diff[:, P * k : P * (k + 1)], neg_mean[h][:, P * k : P * (k + 1)], start=False, stop=(k == 3))
             square[h] = sb("square%d" % h, [P, I], F32)
             nc.scalar.activation(square[h][:], diff[:], ACT.Square)
 
-        def exp_scores(h):
-            score = sb("score%d" % h, [P, I], F32)
+        def turn_plain(h):
+            plain[h] = bank("plain%d" % h, "a%d" % h)
+            for k in range(4):
+                turn(plain[h][:, P * k : P * (k + 1)], a0_sb[h][:, P * k : P * (k + 1)])
+
+        def scores(h):
+            score[h] = sb("score%d" % h, [P, I], F32)
             nc.vector.scalar_tensor_tensor(
-                score[:], plain[h][:], lam2[:, h : h + 1], square[h][:], ALU.mult, ALU.subtract
+                score[h][:], plain[h][:], lam2[:, h : h + 1], square[h][:], ALU.mult, ALU.subtract
             )
-            run_max = sb("run_max%d" % h, [P, 64], F32)
-            nc.vector.tensor_reduce(run_max[:], score[:].rearrange("p (g j) -> p g j", j=8), AX.X, ALU.max)
-            neg_max = sb("neg_max%d" % h, [P, 1], F32)
-            nc.vector.tensor_reduce(neg_max[:], run_max[:], AX.X, ALU.max, negate=True)
+
+        def run_maxima(h):
+            run_max[h] = sb("run_max%d" % h, [P, 64], F32)
+            nc.vector.tensor_reduce(run_max[h][:], score[h][:].rearrange("p (g j) -> p g j", j=8), AX.X, ALU.max)
+
+        def exps(h):
+            neg_max[h] = sb("neg_max%d" % h, [P, 1], F32)
+            nc.vector.tensor_reduce(neg_max[h][:], run_max[h][:], AX.X, ALU.max, negate=True)
             expd[h] = sb("expd%d" % h, [P, 4, P], F32)
             nc.scalar.activation(
                 expd[h][:].rearrange("q r p -> q p r"),
-                score[:].rearrange("q (p r) -> q p r", r=4),
+                score[h][:].rearrange("q (p r) -> q p r", r=4),
                 ACT.Exp,
-                bias=neg_max[:],
+                bias=neg_max[h][:],
             )
-            row_sum[h] = sb("row_sum%d" % h, [P, 1], F32)
-            nc.scalar.activation(run_top[:, h, :], run_max[:], ACT.Exp, bias=neg_max[:], accum_out=row_sum[h][:])
+            run_top[h] = sb("run_top%d" % h, [P, 64], F32)
+            nc.scalar.activation(
+                run_top[h][:], run_max[h][:], ACT.Exp, bias=neg_max[h][:], accum_out=row_sum[:, h : h + 1]
+            )
 
         def sum_runs(h):
             run_sum = sb("run_sum%d" % h, [P, 64], F32)
             nc.vector.tensor_reduce(run_sum[:], expd[h][:].rearrange("q r (g c) -> q g r c", c=2), AX.XY, ALU.add)
-            nc.vector.tensor_scalar(den[:, h, :], run_sum[:], row_sum[h][:], TINY, ALU.mult, ALU.max)
-            e_turned[h] = bank("e_turned%d" % h, "d%d" % h)
+            return run_sum
+
+        def invert(h, run_sum):
+            inv[h] = sb("inv%d" % h, [P, 64], F32)
+            nc.vector.reciprocal(inv[h][:], run_sum[:])
+
+        def turn_exps(h):
+            if h == 0:
+                for b in range(2):
+                    e_turned[b] = bank("e_turned%d" % b, "x%d" % b)
             for r in range(4):
-                turn(e_turned[h][:, P * r : P * (r + 1)], expd[h][:, r, :])
+                c0 = Q * (r % 2) + P * h
+                turn(e_turned[r // 2][:, c0 : c0 + P], expd[h][:, r, :])
 
-        factor = sb("factor", [P, 4, Q], F32)
+        scaled = sb("scaled", [P, 4, Q], F32)
 
-        def run_shares():
-            inv = sb("inv", [P, P], F32)
-            nc.vector.reciprocal(inv[:], den[:].rearrange("q h g -> q (h g)"))
-            share = sb("share", [P, 2 * P], F32)
-            nc.vector.tensor_tensor(
-                share[:].rearrange("q (n c) -> q n c", c=2),
-                run_top[:].rearrange("q h g -> q (h g)").unsqueeze(2).to_broadcast([P, P, 2]),
-                inv[:].unsqueeze(2).to_broadcast([P, P, 2]),
+        def scale_exps():
+            for r in range(4):
+                c0 = Q * (r % 2)
+                nc.scalar.activation(
+                    scaled[:, r, :], e_turned[r // 2][:, c0 : c0 + Q], ACT.Copy, scale=os4[:, r : r + 1]
+                )
+
+        run_part = {}
+
+        def normalise_tops():
+            inv_row = sb("inv_row", [P, 2], F32)
+            nc.vector.reciprocal(inv_row[:], row_sum[:])
+            for h in range(2):
+                run_part[h] = sb("run_part%d" % h, [P, 64], F32)
+                nc.scalar.activation(run_part[h][:], run_top[h][:], ACT.Copy, scale=inv_row[:, h : h + 1])
+
+        share_t = bank("share_t", "s")
+
+        def run_shares(h):
+            share[h] = sb("share%d" % h, [P, P], F32)
+            nc.vector.scalar_tensor_tensor(
+                share[h][:].rearrange("q (g c) -> q g c", c=2),
+                inv[h][:].unsqueeze(2).to_broadcast([P, 64, 2]),
+                HUGE,
+                run_part[h][:].unsqueeze(2).to_broadcast([P, 64, 2]),
+                ALU.min,
                 ALU.mult,
             )
-            share_t = bank("share_t", "a0")
-            for h in range(2):
-                turn(share_t[:, P * h : P * (h + 1)], share[:, P * h : P * (h + 1)])
-            for r in range(4):
-                nc.scalar.activation(factor[:, r, :], share_t[:, 0:Q], ACT.Copy, scale=os4[:, r : r + 1])
+            turn(share_t[:, P * h : P * (h + 1)], share[h][:])
 
-        w_mx = {}
-
-        def weights(half):
-            w_bf = sb("w_bf%d" % half, [P, 2, 64, 4], BF16)
-            for h in range(2):
-                c0 = 64 * half
-                nc.vector.tensor_tensor(
-                    w_bf[:, h, :, :],
-                    e_turned[h][:].rearrange("p (r m) -> p m r", r=4)[:, c0 : c0 + 64, :],
-                    factor[:].rearrange("p r n -> p n r")[:, P * h + c0 : P * h + c0 + 64, :],
-                    ALU.mult,
-                )
+        def weights(h):
+            w_bf = sb("w_bf%d" % h, [P, P, 4], BF16)
+            cols = slice(P * h, P * (h + 1))
+            nc.vector.tensor_tensor(
+                w_bf[:],
+                share_t[:, cols].unsqueeze(2).to_broadcast([P, P, 4]),
+                scaled[:].rearrange("p r n -> p n r")[:, cols, :],
+                ALU.mult,
+            )
             return w_bf
 
-        turn_scores(0)
-        turn_scores(1)
-        gather_values(0)
+        copy_products(0)
+        copy_products(1)
+        gather_values(0, "key_words")
         mean_values(0)
-        gather_values(1)
-        exp_scores(0)
-        exp_scores(1)
-        centre_values(0, False)
+        group_means(0)
+        group_means(1)
+        turn_differences(0)
+        turn_differences(1)
+        turn_plain(1)
+        gather_values(1, "stretch_sum0")
         mean_values(1)
-        sum_runs(0)
-        gather_values(2)
-        sum_runs(1)
-        centre_values(1, False)
-        run_shares()
-        mean_values(2)
-        gather_values(3)
+        gather_values(2, "group_sum1")
+        scores(0)
+        scores(1)
+        centre_values(0, "d0", "neg_mean1", False)
+        run_maxima(0)
+        run_maxima(1)
+        exps(0)
+        exps(1)
+        centre_values(1, "d1", "score1", False)
+        gather_values(3, "square1")
+        mean_values(2, "square0")
+        sums = [sum_runs(0)]
         mean_values(3)
-        centre_values(2, False)
-        w_bf = [weights(half) for half in range(2)]
-        for half in range(2):
-            w_mx[half] = quantise("w%d" % half, w_bf[half][:].rearrange("p h m r -> p (h m r)"), P)
-        for t in range(3):
-            quantise_values(t)
-        centre_values(3, True)
+        sums.append(sum_runs(1))
+        turn_exps(0)
+        turn_exps(1)
+        invert(0, sums[0])
+        normalise_tops()
+        invert(1, sums[1])
+        scale_exps()
+        centre_values(2, "a0", "expd1", False)
+        quantise_values(0, "run_sum0")
+        quantise_values(1, "run_sum1")
+        for h in range(2):
+            run_shares(h)
+        centre_values(3, "a1", "inv1", True)
+        w_bf = [weights(h) for h in range(2)]
+        w_mx = [quantise("w0", w_bf[0][:].rearrange("p m r -> p (m r)"), P)]
         quantise_values(3)
+        quantise_values(2, "scaled")
+        w_mx.append(quantise("w1", w_bf[1][:].rearrange("p m r -> p (m r)"), P))
 
         o_codes = sb("o_codes", [P, Q], I32)
         o_scales = sb("o_scales", [P, Q], U8)
         out_rows = out_0.rearrange("(p t) q -> p t q", t=4)
-        for half in range(2):
-            acc = bank("acc%d" % half, "x%d" % half)
-            for t in range(4):
-                nc.tensor.matmul_mx(
-                    out=acc[:, P * t : P * (t + 1)],
-                    lhsT=v_mx[t][0][:].bitcast(FP8X4),
-                    lhsT_scale=v_mx[t][1][:],
-                    rhs=w_mx[half][0][:].bitcast(FP8X4),
-                    rhs_scale=w_mx[half][1][:],
-                    start=True,
-                    stop=True,
-                )
-            o_sb = sb("o_sb%d" % half, [P, 4, P], F32)
-            nc.scalar.copy(
-                o_sb[:].rearrange("p t (m h) -> p t m h", h=2),
-                acc[:].rearrange("p (t h m) -> p t m h", t=4, h=2),
-            )
-            cols = slice(P * half, P * (half + 1))
+        for h in range(2):
+            o_sb = sb("o_sb%d" % h, [P, 4, P], F32)
+            for pair in range(2):
+                acc = bank("acc%d%d" % (h, pair), ("d0", "d1", "x0", "x1")[2 * h + pair])
+                for t in (2 * pair, 2 * pair + 1):
+                    nc.tensor.matmul_mx(
+                        out=acc[:, P * (t % 2) : P * (t % 2 + 1)],
+                        lhsT=v_mx[t][0].bitcast(FP8X4),
+                        lhsT_scale=v_mx[t][1],
+                        rhs=w_mx[h][0][:].bitcast(FP8X4),
+                        rhs_scale=w_mx[h][1][:],
+                        start=True,
+                        stop=True,
+                    )
+                nc.scalar.copy(o_sb[:, 2 * pair : 2 * pair + 2, :].rearrange("p t q -> p (t q)"), acc[:, 0 : 2 * P])
+            cols = slice(P * h, P * (h + 1))
             nc.sync.dma_start(out_rows[:, :, cols], o_sb[:])
-            o_bf = sb("o_bf%d" % half, [P, P, 4], BF16)
+            o_bf = sb("o_bf%d" % h, [P, P, 4], BF16)
             nc.vector.tensor_copy(
                 o_bf[:].rearrange("p (c i) t -> p c t i", i=4),
                 o_sb[:].rearrange("p t (c i) -> p c t i", i=4),

@@ -20,7 +20,6 @@ AX = mybir.AxisListType
 
 P = 128
 HUGE = 1e30
-POOL_TILES = ()
 
 
 def tile_attend_rowtypical_bestofruns_centredvalues_pl_kernel(
@@ -51,14 +50,13 @@ def tile_attend_rowtypical_bestofruns_centredvalues_pl_kernel(
         nc.sync.dma_start(key_words[:].bitcast(I32), keys_words[0].bitcast(I32))
         val_rows = vals.rearrange("(p t) n -> t p n", t=4)
         val_pool = [sb("val_pool%d" % t, [P, T], F32) for t in range(4)]
-        nc.sync.dma_start(val_pool[0][:], val_rows[0])
+        for t in range(4):
+            nc.sync.dma_start(val_pool[t][:], val_rows[t])
         lam2 = sb("lam2", [P, 2], F32)
         with nc.allow_non_contiguous_dma(reason="one factor for each query row"):
             nc.sync.dma_start(lam2[:], lam.rearrange("o (h p) -> (o p) h", h=2))
         vsc4 = sb("vsc4", [P, 4], F32)
         nc.sync.dma_start(vsc4[:], vsc.rearrange("o (p t) -> (o p) t", t=4))
-        for t in range(1, 4):
-            nc.sync.dma_start(val_pool[t][:], val_rows[t])
         os4 = sb("os4", [P, 4], F32)
         nc.sync.dma_start(os4[:], slot_os.rearrange("o (p t) -> (o p) t", t=4))
 
@@ -128,51 +126,44 @@ def tile_attend_rowtypical_bestofruns_centredvalues_pl_kernel(
             nc.scalar.copy(a0_sb[h][:], a0_banks[h][:])
 
         def group_means(h):
-            group_sum = sb("group_sum%d" % h, [P, 64], F32)
-            nc.vector.tensor_reduce(group_sum[:], a0_banks[h][:].rearrange("p (v j) -> p v j", j=8), AX.X, ALU.add)
+            group_sum = group_sums[:, 64 * h : 64 * (h + 1)]
+            nc.vector.tensor_reduce(group_sum, a0_banks[h][:].rearrange("p (v j) -> p v j", j=8), AX.X, ALU.add)
             neg_mean[h] = sb("neg_mean%d" % h, [P, I], F32)
             nc.scalar.activation(
                 neg_mean[h][:].rearrange("p (v j) -> p v j", j=8),
-                group_sum[:].unsqueeze(2).to_broadcast([P, 64, 8]),
+                group_sum.unsqueeze(2).to_broadcast([P, 64, 8]),
                 ACT.Copy,
                 scale=-0.125,
             )
 
         picked, neg_vmean, v_mx, v_bf = {}, {}, {}, {}
 
-        def gather_values(t, after):
-            picked[t] = sb("picked%d" % t, [P, I], F32, after)
-            nc.vector.tensor_copy(picked[t][:], val_pool[t][:].indirect(offsets[:]))
+        def gather_values(t, out):
+            picked[t] = out
+            nc.vector.tensor_copy(out, val_pool[t][:].indirect(offsets[:]))
 
-        def mean_values(t, after=None):
-            stretch_sum = sb("stretch_sum%d" % t, [P, 32], F32, after)
-            if t in POOL_TILES:
-                part = picked[t]
-                for width in (8, 4, 2, 1):
-                    halves = part[:].rearrange("p (s u j) -> p s u j", u=2, j=width)
-                    part = stretch_sum if width == 1 else sb("part%d_%d" % (t, width), [P, 32 * width], F32)
-                    nc.gpsimd.tensor_tensor(
-                        part[:].rearrange("p (s j) -> p s j", j=width), halves[:, :, 0, :], halves[:, :, 1, :], ALU.add
-                    )
-            else:
-                nc.vector.tensor_reduce(
-                    stretch_sum[:], picked[t][:].rearrange("p (s j) -> p s j", j=16), AX.X, ALU.add
-                )
-            neg_vmean[t] = sb("neg_vmean%d" % t, [P, P], F32)
-            nc.scalar.activation(
-                neg_vmean[t][:].rearrange("p (s j) -> p s j", j=4),
-                stretch_sum[:].unsqueeze(2).to_broadcast([P, 32, 4]),
-                ACT.Copy,
-                scale=-0.0625,
+        def mean_values(tiles, source, after=None):
+            n = 32 * len(tiles)
+            stretch_sum = sb("stretch_sum%d" % tiles[0], [P, n], F32, after)
+            nc.vector.tensor_reduce(stretch_sum[:], source.rearrange("p (s j) -> p s j", j=16), AX.X, ALU.add)
+            spread = sb("neg_vmean%d" % tiles[0], [P, 4 * n], F32)
+            nc.gpsimd.tensor_scalar(
+                spread[:].rearrange("p (s j) -> p s j", j=4),
+                stretch_sum[:].unsqueeze(2).to_broadcast([P, n, 4]),
+                -0.0625,
+                0.0,
+                ALU.mult,
+                ALU.add,
             )
+            for k, t in enumerate(tiles):
+                neg_vmean[t] = spread[:, P * k : P * (k + 1)]
 
-        def centre_values(t, tag, after, on_vector):
+        def centre_values(t, tag, on_vector):
             centred = bank("centred%d" % t, tag)
             for r in range(4):
                 turn(centred[:, P * r : P * (r + 1)], picked[t][:, r:I:4], start=(r == 0), stop=False)
             for r in range(4):
-                turn(centred[:, P * r : P * (r + 1)], neg_vmean[t][:], start=False, stop=(r == 3))
-            v_bf[t] = sb("v_bf%d" % t, [P, P, 4], BF16, after)[:]
+                turn(centred[:, P * r : P * (r + 1)], neg_vmean[t], start=False, stop=(r == 3))
             if on_vector:
                 nc.vector.tensor_tensor(
                     v_bf[t],
@@ -190,8 +181,14 @@ def tile_attend_rowtypical_bestofruns_centredvalues_pl_kernel(
             codes, scales = quantise("v%d" % t, v_bf[t].rearrange("p e r -> p (e r)"), P, after)
             v_mx[t] = (codes[:], scales[:])
 
-        square, score, run_max, neg_max, expd, run_top, e_turned, inv, share = {}, {}, {}, {}, {}, {}, {}, {}, {}
+        def quantise_pair(pair, after):
+            codes, scales = quantise("v01", pair[:].rearrange("p t e r -> p (t e r)"), 2 * P, after)
+            for t in range(2):
+                v_mx[t] = (codes[:, P * t : P * (t + 1)], scales[:, P * t : P * (t + 1)])
+
+        square, score, run_max, neg_max, expd, run_top, e_turned = {}, {}, {}, {}, {}, {}, {}
         row_sum = sb("row_sum", [P, 2], F32)
+        run_sum = sb("run_sum", [P, P], F32)
 
         def turn_differences(h):
             diff = bank("diff%d" % h, "d%d" % h)
@@ -208,14 +205,14 @@ def tile_attend_rowtypical_bestofruns_centredvalues_pl_kernel(
                 turn(plain[h][:, P * k : P * (k + 1)], a0_sb[h][:, P * k : P * (k + 1)])
 
         def scores(h):
-            score[h] = sb("score%d" % h, [P, I], F32)
+            score[h] = both_scores[:, I * h : I * (h + 1)]
             nc.vector.scalar_tensor_tensor(
-                score[h][:], plain[h][:], lam2[:, h : h + 1], square[h][:], ALU.mult, ALU.subtract
+                score[h], plain[h][:], lam2[:, h : h + 1], square[h][:], ALU.mult, ALU.subtract
             )
 
         def run_maxima(h):
             run_max[h] = sb("run_max%d" % h, [P, 64], F32)
-            nc.vector.tensor_reduce(run_max[h][:], score[h][:].rearrange("p (g j) -> p g j", j=8), AX.X, ALU.max)
+            nc.vector.tensor_reduce(run_max[h][:], score[h].rearrange("p (g j) -> p g j", j=8), AX.X, ALU.max)
 
         def exps(h):
             neg_max[h] = sb("neg_max%d" % h, [P, 1], F32)
@@ -223,7 +220,7 @@ def tile_attend_rowtypical_bestofruns_centredvalues_pl_kernel(
             expd[h] = sb("expd%d" % h, [P, 4, P], F32)
             nc.scalar.activation(
                 expd[h][:].rearrange("q r p -> q p r"),
-                score[h][:].rearrange("q (p r) -> q p r", r=4),
+                score[h].rearrange("q (p r) -> q p r", r=4),
                 ACT.Exp,
                 bias=neg_max[h][:],
             )
@@ -233,13 +230,9 @@ def tile_attend_rowtypical_bestofruns_centredvalues_pl_kernel(
             )
 
         def sum_runs(h):
-            run_sum = sb("run_sum%d" % h, [P, 64], F32)
-            nc.vector.tensor_reduce(run_sum[:], expd[h][:].rearrange("q r (g c) -> q g r c", c=2), AX.XY, ALU.add)
-            return run_sum
-
-        def invert(h, run_sum):
-            inv[h] = sb("inv%d" % h, [P, 64], F32)
-            nc.vector.reciprocal(inv[h][:], run_sum[:])
+            nc.vector.tensor_reduce(
+                run_sum[:, 64 * h : 64 * (h + 1)], expd[h][:].rearrange("q r (g c) -> q g r c", c=2), AX.XY, ALU.add
+            )
 
         def turn_exps(h):
             if h == 0:
@@ -258,91 +251,103 @@ def tile_attend_rowtypical_bestofruns_centredvalues_pl_kernel(
                     scaled[:, r, :], e_turned[r // 2][:, c0 : c0 + Q], ACT.Copy, scale=os4[:, r : r + 1]
                 )
 
-        run_part = {}
+        run_part = sb("run_part", [P, P], F32)
 
         def normalise_tops():
             inv_row = sb("inv_row", [P, 2], F32)
             nc.vector.reciprocal(inv_row[:], row_sum[:])
             for h in range(2):
-                run_part[h] = sb("run_part%d" % h, [P, 64], F32)
-                nc.scalar.activation(run_part[h][:], run_top[h][:], ACT.Copy, scale=inv_row[:, h : h + 1])
+                nc.scalar.activation(
+                    run_part[:, 64 * h : 64 * (h + 1)], run_top[h][:], ACT.Copy, scale=inv_row[:, h : h + 1]
+                )
 
-        share_t = bank("share_t", "s")
+        share_t, inv = {}, {}
+
+        def invert(h):
+            inv[h] = sb("inv%d" % h, [P, 64], F32)
+            nc.vector.reciprocal(inv[h][:], run_sum[:, 64 * h : 64 * (h + 1)])
 
         def run_shares(h):
-            share[h] = sb("share%d" % h, [P, P], F32)
+            share = sb("share%d" % h, [P, P], F32)
             nc.vector.scalar_tensor_tensor(
-                share[h][:].rearrange("q (g c) -> q g c", c=2),
+                share[:].rearrange("q (n c) -> q n c", c=2),
                 inv[h][:].unsqueeze(2).to_broadcast([P, 64, 2]),
                 HUGE,
-                run_part[h][:].unsqueeze(2).to_broadcast([P, 64, 2]),
+                run_part[:, 64 * h : 64 * (h + 1)].unsqueeze(2).to_broadcast([P, 64, 2]),
                 ALU.min,
                 ALU.mult,
             )
-            turn(share_t[:, P * h : P * (h + 1)], share[h][:])
+            turn(share_t[h][:, 0:P], share[:])
 
         def weights(h):
             w_bf = sb("w_bf%d" % h, [P, P, 4], BF16)
             cols = slice(P * h, P * (h + 1))
             nc.vector.tensor_tensor(
                 w_bf[:],
-                share_t[:, cols].unsqueeze(2).to_broadcast([P, P, 4]),
+                share_t[h][:, 0:P].unsqueeze(2).to_broadcast([P, P, 4]),
                 scaled[:].rearrange("p r n -> p n r")[:, cols, :],
                 ALU.mult,
             )
             return w_bf
 
-        copy_products(0)
         copy_products(1)
-        gather_values(0, "key_words")
-        mean_values(0)
+        gather_values(0, sb("picked0", [P, I], F32)[:])
+        group_sums = sb("group_sums", [P, P], F32, "val_pool0")
         group_means(0)
+        copy_products(0)
+        mean_values((0,), picked[0])
         group_means(1)
         turn_differences(0)
         turn_differences(1)
         turn_plain(1)
-        gather_values(1, "stretch_sum0")
-        mean_values(1)
-        gather_values(2, "group_sum1")
+        picked12 = sb("picked12", [P, 2 * I], F32)
+        gather_values(1, picked12[:, 0:I])
+        gather_values(2, picked12[:, I : 2 * I])
+        mean_values((1, 2), picked12[:])
+        gather_values(3, sb("picked3", [P, I], F32)[:])
+        both_scores = sb("both_scores", [P, 2 * I], F32, "val_pool3")
         scores(0)
         scores(1)
-        centre_values(0, "d0", "neg_mean1", False)
+        pair = sb("v_bf01", [P, 2, P, 4], BF16)
+        v_bf[0], v_bf[1] = pair[:, 0, :, :], pair[:, 1, :, :]
+        centre_values(0, "v", False)
+        centre_values(1, "d0", False)
         run_maxima(0)
         run_maxima(1)
         exps(0)
         exps(1)
-        centre_values(1, "d1", "score1", False)
-        gather_values(3, "square1")
-        mean_values(2, "square0")
-        sums = [sum_runs(0)]
-        mean_values(3)
-        sums.append(sum_runs(1))
+        mean_values((3,), picked[3], "square1")
+        quantise_pair(pair, "square0")
+        sum_runs(0)
+        sum_runs(1)
         turn_exps(0)
         turn_exps(1)
-        invert(0, sums[0])
         normalise_tops()
-        invert(1, sums[1])
+        invert(0)
+        invert(1)
         scale_exps()
-        centre_values(2, "a0", "expd1", False)
-        quantise_values(0, "run_sum0")
-        quantise_values(1, "run_sum1")
-        for h in range(2):
-            run_shares(h)
-        centre_values(3, "a1", "inv1", True)
+        v_bf[2] = sb("v_bf2", [P, P, 4], BF16, "expd1")[:]
+        centre_values(2, "d1", False)
+        share_t[0] = bank("share_t0", "s")
+        share_t[1] = bank("share_t1", "a1")
+        run_shares(0)
+        run_shares(1)
+        v_bf[3] = sb("v_bf3", [P, P, 4], BF16, "inv1")[:]
+        centre_values(3, "a0", True)
         w_bf = [weights(h) for h in range(2)]
         w_mx = [quantise("w0", w_bf[0][:].rearrange("p m r -> p (m r)"), P)]
         quantise_values(3)
-        quantise_values(2, "scaled")
         w_mx.append(quantise("w1", w_bf[1][:].rearrange("p m r -> p (m r)"), P))
+        quantise_values(2, "scaled")
 
         o_codes = sb("o_codes", [P, Q], I32)
         o_scales = sb("o_scales", [P, Q], U8)
         out_rows = out_0.rearrange("(p t) q -> p t q", t=4)
         for h in range(2):
             o_sb = sb("o_sb%d" % h, [P, 4, P], F32)
-            for pair in range(2):
-                acc = bank("acc%d%d" % (h, pair), ("d0", "d1", "x0", "x1")[2 * h + pair])
-                for t in (2 * pair, 2 * pair + 1):
+            for half in range(2):
+                acc = bank("acc%d%d" % (h, half), ("v", "d0", "x0", "x1")[2 * h + half])
+                for t in (2 * half, 2 * half + 1):
                     nc.tensor.matmul_mx(
                         out=acc[:, P * (t % 2) : P * (t % 2 + 1)],
                         lhsT=v_mx[t][0].bitcast(FP8X4),
@@ -352,7 +357,7 @@ def tile_attend_rowtypical_bestofruns_centredvalues_pl_kernel(
                         start=True,
                         stop=True,
                     )
-                nc.scalar.copy(o_sb[:, 2 * pair : 2 * pair + 2, :].rearrange("p t q -> p (t q)"), acc[:, 0 : 2 * P])
+                nc.scalar.copy(o_sb[:, 2 * half : 2 * half + 2, :].rearrange("p t q -> p (t q)"), acc[:, 0 : 2 * P])
             cols = slice(P * h, P * (h + 1))
             nc.sync.dma_start(out_rows[:, :, cols], o_sb[:])
             o_bf = sb("o_bf%d" % h, [P, P, 4], BF16)

from contextlib import ExitStack

import concourse.mybir as mybir
from concourse.masks import make_identity

D, T, I, Q, E = 512, 2048, 512, 256, 512
FLOPS = 2 * D * I * Q + 2 * I * E * Q

F32 = mybir.dt.float32
BF16 = mybir.dt.bfloat16
I32 = mybir.dt.int32
U32 = mybir.dt.uint32
U16 = mybir.dt.uint16
U8 = mybir.dt.uint8
FP8X4 = mybir.dt.float8_e4m3fn_x4
FP4X4 = mybir.dt.float4_e2m1fn_x4
ALU = mybir.AluOpType
ACT = mybir.ActivationFunctionType
AX = mybir.AxisListType

P = 128
HUGE = 1e30


def tile_attend_rowtypical_bestofruns_centredvalues_pl_kernel(
    tc, query, keys_words, keys_scales, lam, slot_os, vals, vsc, offs, out_0, out_1, out_2
):
    nc = tc.nc
    with ExitStack() as ctx:
        keep = ctx.enter_context(tc.tile_pool(name="keep", bufs=1))
        psum = ctx.enter_context(tc.psum_pool(name="psum", bufs=1))

        def sb(name, shape, dtype, after=None):
            return keep.tile(shape, dtype, name=name, tag=after or name, align_bytes=64)

        def bank(name, tag):
            return psum.tile([P, 512], F32, name=name, tag=tag)

        offsets = keep.tile([P, I // 16], U16, name="offsets")
        nc.sync.dma_start(offsets[:], offs)
        staged_bytes = sb("staged_bytes", [P, T // 4], I32)
        for quad in range(4):
            nc.sync.dma_start(
                staged_bytes[32 * quad : 32 * quad + 4, :],
                keys_scales[0, 4 * quad : 4 * quad + 4, :].bitcast(I32),
            )
        q_raw = sb("q_raw", [P, 4, Q], F32)
        nc.sync.dma_start(q_raw[:], query.rearrange("(p j) q -> p j q", j=4))
        key_words = sb("key_words", [P, T], U16)
        nc.sync.dma_start(key_words[:].bitcast(I32), keys_words[0].bitcast(I32))
        val_rows = vals.rearrange("(p t) n -> t p n", t=4)
        val_pool = [sb("val_pool%d" % t, [P, T], F32) for t in range(4)]
        for t in range(4):
            nc.sync.dma_start(val_pool[t][:], val_rows[t])
        lam2 = sb("lam2", [P, 2], F32)
        with nc.allow_non_contiguous_dma(reason="one factor for each query row"):
            nc.sync.dma_start(lam2[:], lam.rearrange("o (h p) -> (o p) h", h=2))
        vsc4 = sb("vsc4", [P, 4], F32)
        nc.sync.dma_start(vsc4[:], vsc.rearrange("o (p t) -> (o p) t", t=4))
        os4 = sb("os4", [P, 4], F32)
        nc.sync.dma_start(os4[:], slot_os.rearrange("o (p t) -> (o p) t", t=4))

        ident = sb("ident", [P, P], F32)
        make_identity(nc, ident[:])

        key_bytes = sb("key_bytes", [P, T], U8)
        nc.vector.memset(key_bytes[:].bitcast(I32), 0)
        warm_in = sb("warm_in", [P, 1], F32)
        warm_out = sb("warm_out", [P, 1], F32)
        nc.vector.memset(warm_in[:], 0.0)
        nc.scalar.activation(warm_out[:], warm_in[:], ACT.Exp)

        def turn(out, in_, start=True, stop=True):
            nc.tensor.matmul(out, lhsT=in_, rhs=ident[:], is_transpose=True, start=start, stop=stop)

        def quantise(name, grouped, width, after=None):
            codes = sb(name + "_codes", [P, width], U32, after)
            scales = sb(name + "_scales", [P, width], U8)
            nc.vector.quantize_mx(out=codes[:].bitcast(FP8X4), scales=scales[:], in_=grouped)
            return codes, scales

        for quad in range(4):
            rows = slice(32 * quad, 32 * quad + 4)
            nc.vector.tensor_copy(key_bytes[rows, :].bitcast(I32), staged_bytes[rows, :])
        kb_g = sb("kb_g", [P, I], U8)
        nc.vector.tensor_copy(kb_g[:], key_bytes[:].indirect(offsets[:]))
        kw_g = [sb("kw_g0", [P, I // 2], U16)]
        nc.vector.tensor_copy(kw_g[0][:], key_words[:].indirect(offsets[:, 0:16]))

        q_bf = sb("q_bf", [P, Q, 4], BF16)
        nc.scalar.copy(
            q_bf[:].rearrange("p (c i) t -> p c t i", i=4),
            q_raw[:].rearrange("p t (c i) -> p c t i", i=4),
        )
        q_codes, q_scales = quantise("q", q_bf[:].rearrange("p q t -> p (q t)"), Q)
        kw_g.append(sb("kw_g1", [P, I // 2], U16, "q_bf"))
        nc.vector.tensor_copy(kw_g[1][:], key_words[:].indirect(offsets[:, 16:32]))

        a0_banks, a0_sb, neg_mean, plain = {}, {}, {}, {}
        for h in range(2):
            a0_banks[h] = bank("a0_%d" % h, "x%d" % h)
            for k in range(4):
                nc.tensor.matmul_mx(
                    out=a0_banks[h][:, P * k : P * (k + 1)],
                    lhsT=kw_g[k // 2][:, P * (k % 2) : P * (k % 2 + 1)].bitcast(FP4X4),
                    lhsT_scale=kb_g[:, P * k : P * (k + 1)],
                    rhs=q_codes[:, P * h : P * (h + 1)].bitcast(FP8X4),
                    rhs_scale=q_scales[:, P * h : P * (h + 1)],
                    start=True,
                    stop=True,
                )
        plain[0] = bank("plain0", "a0")
        for b in range(2):
            nc.tensor.matmul_mx(
                out=plain[0][:, Q * b : Q * (b + 1)],
                lhsT=q_codes[:, 0:P].bitcast(FP8X4),
                lhsT_scale=q_scales[:, 0:P],
                rhs=kw_g[b][:].bitcast(FP4X4),
                rhs_scale=kb_g[:, Q * b : Q * (b + 1)],
                start=True,
                stop=True,
            )

        def copy_products(h):
            a0_sb[h] = sb("a0_sb%d" % h, [P, I], F32)
            nc.scalar.copy(a0_sb[h][:], a0_banks[h][:])

        def group_means(h):
            group_sum = group_sums[:, 64 * h : 64 * (h + 1)]
            nc.vector.tensor_reduce(group_sum, a0_banks[h][:].rearrange("p (v j) -> p v j", j=8), AX.X, ALU.add)
            neg_mean[h] = sb("neg_mean%d" % h, [P, I], F32)
            nc.scalar.activation(
                neg_mean[h][:].rearrange("p (v j) -> p v j", j=8),
                group_sum.unsqueeze(2).to_broadcast([P, 64, 8]),
                ACT.Copy,
                scale=-0.125,
            )

        picked, neg_vmean, v_mx, v_bf = {}, {}, {}, {}

        def gather_values(t, out):
            picked[t] = out
            nc.vector.tensor_copy(out, val_pool[t][:].indirect(offsets[:]))

        def mean_values(tiles, source, after=None):
            n = 32 * len(tiles)
            stretch_sum = sb("stretch_sum%d" % tiles[0], [P, n], F32, after)
            nc.vector.tensor_reduce(stretch_sum[:], source.rearrange("p (s j) -> p s j", j=16), AX.X, ALU.add)
            spread = sb("neg_vmean%d" % tiles[0], [P, 4 * n], F32)
            nc.gpsimd.tensor_scalar(
                spread[:].rearrange("p (s j) -> p s j", j=4),
                stretch_sum[:].unsqueeze(2).to_broadcast([P, n, 4]),
                -0.0625,
                0.0,
                ALU.mult,
                ALU.add,
            )
            for k, t in enumerate(tiles):
                neg_vmean[t] = spread[:, P * k : P * (k + 1)]

        def centre_values(t, tag, on_vector):
            centred = bank("centred%d" % t, tag)
            for r in range(4):
                turn(centred[:, P * r : P * (r + 1)], picked[t][:, r:I:4], start=(r == 0), stop=False)
            for r in range(4):
                turn(centred[:, P * r : P * (r + 1)], neg_vmean[t], start=False, stop=(r == 3))
            if on_vector:
                nc.vector.tensor_tensor(
                    v_bf[t],
                    centred[:].rearrange("p (r e) -> p e r", r=4),
                    vsc4[:].unsqueeze(1).to_broadcast([P, P, 4]),
                    ALU.mult,
                )
            else:
                for r in range(4):
                    nc.scalar.activation(
                        v_bf[t][:, :, r], centred[:, P * r : P * (r + 1)], ACT.Copy, scale=vsc4[:, r : r + 1]
                    )

        def quantise_values(t, after=None):
            codes, scales = quantise("v%d" % t, v_bf[t].rearrange("p e r -> p (e r)"), P, after)
            v_mx[t] = (codes[:], scales[:])

        def quantise_pair(pair, after):
            codes, scales = quantise("v01", pair[:].rearrange("p t e r -> p (t e r)"), 2 * P, after)
            for t in range(2):
                v_mx[t] = (codes[:, P * t : P * (t + 1)], scales[:, P * t : P * (t + 1)])

        square, score, run_max, neg_max, expd, run_top, e_turned = {}, {}, {}, {}, {}, {}, {}
        row_sum = sb("row_sum", [P, 2], F32)
        run_sum = sb("run_sum", [P, P], F32)

        def turn_differences(h):
            diff = bank("diff%d" % h, "d%d" % h)
            for k in range(4):
                turn(diff[:, P * k : P * (k + 1)], a0_sb[h][:, P * k : P * (k + 1)], start=(k == 0), stop=False)
            for k in range(4):
                turn(diff[:, P * k : P * (k + 1)], neg_mean[h][:, P * k : P * (k + 1)], start=False, stop=(k == 3))
            square[h] = sb("square%d" % h, [P, I], F32)
            nc.scalar.activation(square[h][:], diff[:], ACT.Square)

        def turn_plain(h):
            plain[h] = bank("plain%d" % h, "a%d" % h)
            for k in range(4):
                turn(plain[h][:, P * k : P * (k + 1)], a0_sb[h][:, P * k : P * (k + 1)])

        def scores(h):
            score[h] = both_scores[:, I * h : I * (h + 1)]
            nc.vector.scalar_tensor_tensor(
                score[h], plain[h][:], lam2[:, h : h + 1], square[h][:], ALU.mult, ALU.subtract
            )

        def run_maxima(h):
            run_max[h] = sb("run_max%d" % h, [P, 64], F32)
            nc.vector.tensor_reduce(run_max[h][:], score[h].rearrange("p (g j) -> p g j", j=8), AX.X, ALU.max)

        def exps(h):
            neg_max[h] = sb("neg_max%d" % h, [P, 1], F32)
            nc.vector.tensor_reduce(neg_max[h][:], run_max[h][:], AX.X, ALU.max, negate=True)
            expd[h] = sb("expd%d" % h, [P, 4, P], F32)
            nc.scalar.activation(
                expd[h][:].rearrange("q r p -> q p r"),
                score[h].rearrange("q (p r) -> q p r", r=4),
                ACT.Exp,
                bias=neg_max[h][:],
            )
            run_top[h] = sb("run_top%d" % h, [P, 64], F32)
            nc.scalar.activation(
                run_top[h][:], run_max[h][:], ACT.Exp, bias=neg_max[h][:], accum_out=row_sum[:, h : h + 1]
            )

        def sum_runs(h):
            nc.vector.tensor_reduce(
                run_sum[:, 64 * h : 64 * (h + 1)], expd[h][:].rearrange("q r (g c) -> q g r c", c=2), AX.XY, ALU.add
            )

        def turn_exps(h):
            if h == 0:
                for b in range(2):
                    e_turned[b] = bank("e_turned%d" % b, "x%d" % b)
            for r in range(4):
                c0 = Q * (r % 2) + P * h
                turn(e_turned[r // 2][:, c0 : c0 + P], expd[h][:, r, :])

        scaled = sb("scaled", [P, 4, Q], F32)

        def scale_exps():
            for r in range(4):
                c0 = Q * (r % 2)
                nc.scalar.activation(
                    scaled[:, r, :], e_turned[r // 2][:, c0 : c0 + Q], ACT.Copy, scale=os4[:, r : r + 1]
                )

        run_part = sb("run_part", [P, P], F32)

        def normalise_tops():
            inv_row = sb("inv_row", [P, 2], F32)
            nc.vector.reciprocal(inv_row[:], row_sum[:])
            for h in range(2):
                nc.scalar.activation(
                    run_part[:, 64 * h : 64 * (h + 1)], run_top[h][:], ACT.Copy, scale=inv_row[:, h : h + 1]
                )

        share_t, inv = {}, {}

        def invert(h):
            inv[h] = sb("inv%d" % h, [P, 64], F32)
            nc.vector.reciprocal(inv[h][:], run_sum[:, 64 * h : 64 * (h + 1)])

        def run_shares(h):
            share = sb("share%d" % h, [P, P], F32)
            nc.vector.scalar_tensor_tensor(
                share[:].rearrange("q (n c) -> q n c", c=2),
                inv[h][:].unsqueeze(2).to_broadcast([P, 64, 2]),
                HUGE,
                run_part[:, 64 * h : 64 * (h + 1)].unsqueeze(2).to_broadcast([P, 64, 2]),
                ALU.min,
                ALU.mult,
            )
            turn(share_t[h][:, 0:P], share[:])

        def weights(h):
            w_bf = sb("w_bf%d" % h, [P, P, 4], BF16)
            cols = slice(P * h, P * (h + 1))
            nc.vector.tensor_tensor(
                w_bf[:],
                share_t[h][:, 0:P].unsqueeze(2).to_broadcast([P, P, 4]),
                scaled[:].rearrange("p r n -> p n r")[:, cols, :],
                ALU.mult,
            )
            return w_bf

        copy_products(1)
        gather_values(0, sb("picked0", [P, I], F32)[:])
        group_sums = sb("group_sums", [P, P], F32, "val_pool0")
        group_means(0)
        copy_products(0)
        mean_values((0,), picked[0])
        group_means(1)
        turn_differences(0)
        turn_differences(1)
        turn_plain(1)
        picked12 = sb("picked12", [P, 2 * I], F32)
        gather_values(1, picked12[:, 0:I])
        gather_values(2, picked12[:, I : 2 * I])
        mean_values((1, 2), picked12[:])
        gather_values(3, sb("picked3", [P, I], F32)[:])
        both_scores = sb("both_scores", [P, 2 * I], F32, "val_pool3")
        scores(0)
        scores(1)
        pair = sb("v_bf01", [P, 2, P, 4], BF16)
        v_bf[0], v_bf[1] = pair[:, 0, :, :], pair[:, 1, :, :]
        centre_values(0, "v", False)
        centre_values(1, "d0", False)
        run_maxima(0)
        run_maxima(1)
        exps(0)
        exps(1)
        mean_values((3,), picked[3], "square1")
        quantise_pair(pair, "square0")
        sum_runs(0)
        sum_runs(1)
        turn_exps(0)
        turn_exps(1)
        normalise_tops()
        invert(0)
        invert(1)
        scale_exps()
        v_bf[2] = sb("v_bf2", [P, P, 4], BF16, "expd1")[:]
        centre_values(2, "d1", False)
        share_t[0] = bank("share_t0", "s")
        share_t[1] = bank("share_t1", "a1")
        run_shares(0)
        run_shares(1)
        v_bf[3] = sb("v_bf3", [P, P, 4], BF16, "inv1")[:]
        centre_values(3, "a0", True)
        w_bf = [weights(h) for h in range(2)]
        w_mx = [quantise("w0", w_bf[0][:].rearrange("p m r -> p (m r)"), P)]
        quantise_values(3)
        w_mx.append(quantise("w1", w_bf[1][:].rearrange("p m r -> p (m r)"), P))
        quantise_values(2, "scaled")

        o_codes = sb("o_codes", [P, Q], I32)
        o_scales = sb("o_scales", [P, Q], U8)
        out_rows = out_0.rearrange("(p t) q -> p t q", t=4)
        for h in range(2):
            o_sb = sb("o_sb%d" % h, [P, 4, P], F32)
            for half in range(2):
                acc = bank("acc%d%d" % (h, half), ("v", "d0", "x0", "x1")[2 * h + half])
                for t in (2 * half, 2 * half + 1):
                    nc.tensor.matmul_mx(
                        out=acc[:, P * (t % 2) : P * (t % 2 + 1)],
                        lhsT=v_mx[t][0].bitcast(FP8X4),
                        lhsT_scale=v_mx[t][1],
                        rhs=w_mx[h][0][:].bitcast(FP8X4),
                        rhs_scale=w_mx[h][1][:],
                        start=True,
                        stop=True,
                    )
                nc.scalar.copy(o_sb[:, 2 * half : 2 * half + 2, :].rearrange("p t q -> p (t q)"), acc[:, 0 : 2 * P])
            cols = slice(P * h, P * (h + 1))
            nc.sync.dma_start(out_rows[:, :, cols], o_sb[:])
            o_bf = sb("o_bf%d" % h, [P, P, 4], BF16)
            nc.vector.tensor_copy(
                o_bf[:].rearrange("p (c i) t -> p c t i", i=4),
                o_sb[:].rearrange("p t (c i) -> p c t i", i=4),
            )
            nc.vector.quantize_mx(
                out=o_codes[:, cols].bitcast(FP8X4),
                scales=o_scales[:, cols],
                in_=o_bf[:].rearrange("p q t -> p (q t)"),
            )
        nc.sync.dma_start(out_1[0].rearrange("p c r -> p (c r)").bitcast(I32), o_codes[:])
        for quad in range(4):
            queue = nc.scalar if quad % 2 else nc.sync
            queue.dma_start(
                out_2[0, 4 * quad : 4 * quad + 4, :].bitcast(I32),
                o_scales[32 * quad : 32 * quad + 4, :].bitcast(I32),
            )
